import numpy as np, ml_dtypes
CORES = [125,127,253,255,381,383,509,511]
N = 8
TK, LAY = 128, 3
def setup_inputs(rng):
    return {"x": rng.standard_normal((N, 128, TK), dtype=np.float32).astype(ml_dtypes.bfloat16), "w": (rng.standard_normal((N, 128, LAY * 256), dtype=np.float32) / 16).astype(ml_dtypes.bfloat16)}
def setup_inputs_big(rng):
    d = setup_inputs(rng)
    for k in ("x",): d[k] = (d[k].astype(np.float32) * 1048576.0).astype(d[k].dtype)
    return d
def setup_inputs_small(rng):
    d = setup_inputs(rng)
    for k in ("x",): d[k] = (d[k].astype(np.float32) * (1 / 1048576.0)).astype(d[k].dtype)
    return d
def setup_inputs_apart(rng):
    d = setup_inputs(rng)
    f = (10.0 ** rng.permutation(np.linspace(-1.5, 1.5, N))).astype(np.float32).reshape(N, 1, 1)
    for k in ("x",): d[k] = (d[k].astype(np.float32) * f).astype(d[k].dtype)
    return d
def reference(x, w):
    X, W = x.astype(np.float64), w.astype(np.float64)
    h = list(X)
    for l in range(LAY):
        h = [np.maximum(W[r][:, 256 * l:256 * l + 128].T @ h[r] + W[r][:, 256 * l + 128:256 * l + 256].T @ h[r ^ (1 << l)], 0.0) for r in range(N)]
    return {"y": np.stack(h).astype(ml_dtypes.bfloat16)}

@@ -1,0 +1,104 @@
+from concourse.mybir import AluOpType
+
+TK = 128
+
+SCRATCH = {
+    "xs": ("sbuf", [128, TK], "bfloat16"),
+    "ws": ("sbuf", [128, 6 * TK], "bfloat16"),
+    "wq": ("sbuf", [128, 2 * TK], "bfloat16"),
+    "p0": ("sbuf", [128, TK], "bfloat16"),
+    "p1": ("sbuf", [128, TK], "bfloat16"),
+    "p2": ("sbuf", [128, TK], "bfloat16"),
+    "h1": ("sbuf", [128, TK], "bfloat16"),
+    "h2": ("sbuf", [128, TK], "bfloat16"),
+    "h2q": ("sbuf", [128, TK], "bfloat16"),
+    "yb": ("sbuf", [128, TK], "bfloat16"),
+    "zero": ("sbuf", [128, TK], "float32"),
+    "ps0": ("psum", [128, 512], "float32"),
+    "ps1": ("psum", [128, 512], "float32"),
+    "ps1q": ("psum", [128, 512], "float32"),
+    "ps2": ("psum", [128, 512], "float32"),
+}
+SEMAPHORES = ["ld_x", "ld_w01", "ld_w2", "fill", "left",
+              "in_x", "in_w", "in_h1", "in_h2",
+              "mm0", "mm1", "mm1q", "mm2",
+              "ok_h1", "ok_h2", "ok_h2q", "ok_y", "st_y"]
+
+
+def _count(mask):
+    n = 0
+    while mask:
+        n += mask & 1
+        mask >>= 1
+    return n
+
+
+def rank_program(g, core, T, topo):
+    r = T.rank_of(core)
+    if r is None:
+        return
+    cores, S = T.cores, T.sem
+    near, side, far = cores[r ^ 1], cores[r ^ 2], cores[r ^ 4]
+    assert not topo.may_write(far, core)
+    fed = cores[r ^ 4 ^ 2]
+    assert topo.may_write(core, fed) and topo.may_write(core, side) and topo.may_write(core, near)
+
+    m_side, m_fed = topo.mask(core, side), topo.mask(core, fed)
+    m_near = topo.mask(core, near) & m_side
+    n_near, n_side, n_fed = _count(m_near), _count(m_side), _count(m_fed)
+
+    def send(dst, out, src, sem, mask):
+        rid, pid = topo.addr(dst, core)
+        g.remote_dma(out_ap=out, in_ap=src, remote_sem=sem, local_sem=S.left, pid=pid, routing_id=rid,
+                     dma_engine_mask=mask)
+
+    def W(k):
+        return T.ws[:, k * TK:(k + 1) * TK]
+
+    te, ve = g.tensor, g.vector
+
+    g.sync.dma_start(T.xs[:], T.x[:]).then_inc(S.ld_x, 16)
+    g.scalar.dma_start(T.ws[:, 0:4 * TK], T.w[:, 0:4 * TK]).then_inc(S.ld_w01, 16)
+    g.sync.dma_start(T.ws[:, 4 * TK:6 * TK], T.w[:, 4 * TK:6 * TK]).then_inc(S.ld_w2, 16)
+    ve.memset(T.zero[:], 0.0).then_inc(S.fill, 1)
+
+    g.wait_ge(S.ld_x, 16)
+    send(near, T.p0[:], T.xs[:], S.in_x, m_near)
+    g.wait_ge(S.ld_w01, 16)
+    send(side, T.wq[:], T.ws[:, 2 * TK:4 * TK], S.in_w, m_side)
+    g.wait_ge(S.ok_h1, 1)
+    send(side, T.p1[:], T.h1[:], S.in_h1, m_side)
+    g.wait_ge(S.ok_h2q, 1)
+    send(fed, T.p2[:], T.h2q[:], S.in_h2, m_fed)
+
+    ps0, ps1, ps1q, ps2 = T.ps0[:, 0:TK], T.ps1[:, 0:TK], T.ps1q[:, 0:TK], T.ps2[:, 0:TK]
+    te.wait_ge(S.ld_x, 16)
+    te.wait_ge(S.ld_w01, 16)
+    te.matmul(ps0, W(0), T.xs[:], start=True, stop=False)
+    te.wait_ge(S.in_x, n_near)
+    te.matmul(ps0, W(1), T.p0[:], start=False, stop=True).then_inc(S.mm0, 1)
+
+    te.wait_ge(S.ok_h1, 1)
+    te.matmul(ps1, W(2), T.h1[:], start=True, stop=False)
+    te.wait_ge(S.in_w, n_side)
+    te.matmul(ps1q, T.wq[:, TK:2 * TK], T.h1[:], start=True, stop=False)
+    te.wait_ge(S.in_h1, n_side)
+    te.matmul(ps1q, T.wq[:, 0:TK], T.p1[:], start=False, stop=True).then_inc(S.mm1q, 1)
+    te.matmul(ps1, W(3), T.p1[:], start=False, stop=True).then_inc(S.mm1, 1)
+
+    te.wait_ge(S.ok_h2, 1)
+    te.wait_ge(S.ld_w2, 16)
+    te.matmul(ps2, W(4), T.h2[:], start=True, stop=False)
+    te.wait_ge(S.in_h2, n_fed)
+    te.matmul(ps2, W(5), T.p2[:], start=False, stop=True).then_inc(S.mm2, 1)
+
+    ve.wait_ge(S.fill, 1)
+    for mm, ps, out, ok in ((S.mm0, ps0, T.h1, S.ok_h1), (S.mm1q, ps1q, T.h2q, S.ok_h2q),
+                            (S.mm1, ps1, T.h2, S.ok_h2), (S.mm2, ps2, T.yb, S.ok_y)):
+        ve.wait_ge(mm, 1)
+        ve.tensor_tensor(out=out[:], in0=ps, in1=T.zero[:], op=AluOpType.max).then_inc(ok, 1)
+
+    g.sync.wait_ge(S.ok_y, 1)
+    g.sync.dma_start(T.y[:], T.yb[:]).then_inc(S.st_y, 16)
+    g.sync.wait_ge(S.st_y, 16)
+    g.wait_ge(S.left, n_near + 2 * n_side + n_fed)

@@ -1,6 +1,8 @@
 from concourse.mybir import AluOpType
 
 TK = 128
+NC = 2
+CW = TK // NC
 
 SCRATCH = {
     "xs": ("sbuf", [128, TK], "bfloat16"),
@@ -13,16 +15,14 @@ SCRATCH = {
     "h2": ("sbuf", [128, TK], "bfloat16"),
     "h2q": ("sbuf", [128, TK], "bfloat16"),
     "yb": ("sbuf", [128, TK], "bfloat16"),
-    "zero": ("sbuf", [128, TK], "float32"),
-    "ps0": ("psum", [128, 512], "float32"),
-    "ps1": ("psum", [128, 512], "float32"),
-    "ps1q": ("psum", [128, 512], "float32"),
-    "ps2": ("psum", [128, 512], "float32"),
+    "zero": ("sbuf", [128, CW], "float32"),
 }
-SEMAPHORES = ["ld_x", "ld_w01", "ld_w2", "fill", "left",
-              "in_x", "in_w", "in_h1", "in_h2",
-              "mm0", "mm1", "mm1q", "mm2",
-              "ok_h1", "ok_h2", "ok_h2q", "ok_y", "st_y"]
+SEMAPHORES = ["ld_x", "ld_w01", "ld_w2", "fill", "left", "in_w"]
+for _c in range(NC):
+    for _n in ("ps0", "ps1", "ps1q"):
+        SCRATCH["%s_%d" % (_n, _c)] = ("psum", [128, 512], "float32")
+    for _n in ("in_x", "in_h1", "in_h2", "mm0", "mm1", "mm1q", "mm2", "ok_h1", "ok_h2", "ok_h2q", "ok_y", "st_y"):
+        SEMAPHORES.append("%s_%d" % (_n, _c))
 
 
 def _count(mask):
@@ -55,7 +55,17 @@ def rank_program(g, core, T, topo):
     def W(k):
         return T.ws[:, k * TK:(k + 1) * TK]
 
+    def sem(name, c):
+        return S["%s_%d" % (name, c)]
+
+    def col(t, c):
+        return t[:, c * CW:(c + 1) * CW]
+
+    def ps(name, c):
+        return T["%s_%d" % (name, c)][:, 0:CW]
+
     te, ve = g.tensor, g.vector
+    blocks = range(NC)
 
     g.sync.dma_start(T.xs[:], T.x[:]).then_inc(S.ld_x, 16)
     g.scalar.dma_start(T.ws[:, 0:4 * TK], T.w[:, 0:4 * TK]).then_inc(S.ld_w01, 16)
@@ -63,42 +73,60 @@ def rank_program(g, core, T, topo):
     ve.memset(T.zero[:], 0.0).then_inc(S.fill, 1)
 
     g.wait_ge(S.ld_x, 16)
-    send(near, T.p0[:], T.xs[:], S.in_x, m_near)
+    for c in blocks:
+        send(near, col(T.p0, c), col(T.xs, c), sem("in_x", c), m_near)
     g.wait_ge(S.ld_w01, 16)
     send(side, T.wq[:], T.ws[:, 2 * TK:4 * TK], S.in_w, m_side)
-    g.wait_ge(S.ok_h1, 1)
-    send(side, T.p1[:], T.h1[:], S.in_h1, m_side)
-    g.wait_ge(S.ok_h2q, 1)
-    send(fed, T.p2[:], T.h2q[:], S.in_h2, m_fed)
+    for c in blocks:
+        g.wait_ge(sem("ok_h1", c), 1)
+        send(side, col(T.p1, c), col(T.h1, c), sem("in_h1", c), m_side)
+    for c in blocks:
+        g.wait_ge(sem("ok_h2q", c), 1)
+        send(fed, col(T.p2, c), col(T.h2q, c), sem("in_h2", c), m_fed)
 
-    ps0, ps1, ps1q, ps2 = T.ps0[:, 0:TK], T.ps1[:, 0:TK], T.ps1q[:, 0:TK], T.ps2[:, 0:TK]
     te.wait_ge(S.ld_x, 16)
     te.wait_ge(S.ld_w01, 16)
-    te.matmul(ps0, W(0), T.xs[:], start=True, stop=False)
-    te.wait_ge(S.in_x, n_near)
-    te.matmul(ps0, W(1), T.p0[:], start=False, stop=True).then_inc(S.mm0, 1)
+    for c in blocks:
+        te.matmul(ps("ps0", c), W(0), col(T.xs, c), start=True, stop=False)
+    for c in blocks:
+        te.wait_ge(sem("in_x", c), n_near)
+        te.matmul(ps("ps0", c), W(1), col(T.p0, c), start=False, stop=True).then_inc(sem("mm0", c), 1)
 
-    te.wait_ge(S.ok_h1, 1)
-    te.matmul(ps1, W(2), T.h1[:], start=True, stop=False)
+    for c in blocks:
+        te.wait_ge(sem("ok_h1", c), 1)
+        te.matmul(ps("ps1", c), W(2), col(T.h1, c), start=True, stop=False)
     te.wait_ge(S.in_w, n_side)
-    te.matmul(ps1q, T.wq[:, TK:2 * TK], T.h1[:], start=True, stop=False)
-    te.wait_ge(S.in_h1, n_side)
-    te.matmul(ps1q, T.wq[:, 0:TK], T.p1[:], start=False, stop=True).then_inc(S.mm1q, 1)
-    te.matmul(ps1, W(3), T.p1[:], start=False, stop=True).then_inc(S.mm1, 1)
+    for c in blocks:
+        te.matmul(ps("ps1q", c), T.wq[:, TK:2 * TK], col(T.h1, c), start=True, stop=False)
+    for c in blocks:
+        te.wait_ge(sem("in_h1", c), n_side)
+        te.matmul(ps("ps1q", c), T.wq[:, 0:TK], col(T.p1, c), start=False, stop=True).then_inc(sem("mm1q", c), 1)
+        te.matmul(ps("ps1", c), W(3), col(T.p1, c), start=False, stop=True).then_inc(sem("mm1", c), 1)
 
-    te.wait_ge(S.ok_h2, 1)
     te.wait_ge(S.ld_w2, 16)
-    te.matmul(ps2, W(4), T.h2[:], start=True, stop=False)
-    te.wait_ge(S.in_h2, n_fed)
-    te.matmul(ps2, W(5), T.p2[:], start=False, stop=True).then_inc(S.mm2, 1)
+    for c in blocks:
+        te.wait_ge(sem("ok_h2", c), 1)
+        te.matmul(ps("ps0", c), W(4), col(T.h2, c), start=True, stop=False)
+    for c in blocks:
+        te.wait_ge(sem("in_h2", c), n_fed)
+        te.matmul(ps("ps0", c), W(5), col(T.p2, c), start=False, stop=True).then_inc(sem("mm2", c), 1)
+
+    def relu(mm, p, out, ok, c):
+        ve.wait_ge(sem(mm, c), 1)
+        ve.tensor_tensor(out=col(out, c), in0=ps(p, c), in1=T.zero[:], op=AluOpType.max).then_inc(sem(ok, c), 1)
 
     ve.wait_ge(S.fill, 1)
-    for mm, ps, out, ok in ((S.mm0, ps0, T.h1, S.ok_h1), (S.mm1q, ps1q, T.h2q, S.ok_h2q),
-                            (S.mm1, ps1, T.h2, S.ok_h2), (S.mm2, ps2, T.yb, S.ok_y)):
-        ve.wait_ge(mm, 1)
-        ve.tensor_tensor(out=out[:], in0=ps, in1=T.zero[:], op=AluOpType.max).then_inc(ok, 1)
+    for c in blocks:
+        relu("mm0", "ps0", T.h1, "ok_h1", c)
+    for c in blocks:
+        relu("mm1q", "ps1q", T.h2q, "ok_h2q", c)
+        relu("mm1", "ps1", T.h2, "ok_h2", c)
+    for c in blocks:
+        relu("mm2", "ps0", T.yb, "ok_y", c)
 
-    g.sync.wait_ge(S.ok_y, 1)
-    g.sync.dma_start(T.y[:], T.yb[:]).then_inc(S.st_y, 16)
-    g.sync.wait_ge(S.st_y, 16)
-    g.wait_ge(S.left, n_near + 2 * n_side + n_fed)
+    for c in blocks:
+        q = (g.sync, g.scalar)[c % 2]
+        q.wait_ge(sem("ok_y", c), 1)
+        q.dma_start(col(T.y, c), col(T.yb, c)).then_inc(sem("st_y", c), 16)
+        q.wait_ge(sem("st_y", c), 16)
+    g.wait_ge(S.left, NC * (n_near + n_side + n_fed) + n_side)

from concourse.mybir import AluOpType

TK = 128
NC = 2
CW = TK // NC

SCRATCH = {
    "xs": ("sbuf", [128, TK], "bfloat16"),
    "ws": ("sbuf", [128, 6 * TK], "bfloat16"),
    "wq": ("sbuf", [128, 2 * TK], "bfloat16"),
    "p0": ("sbuf", [128, TK], "bfloat16"),
    "p1": ("sbuf", [128, TK], "bfloat16"),
    "p2": ("sbuf", [128, TK], "bfloat16"),
    "h1": ("sbuf", [128, TK], "bfloat16"),
    "h2": ("sbuf", [128, TK], "bfloat16"),
    "h2q": ("sbuf", [128, TK], "bfloat16"),
    "yb": ("sbuf", [128, TK], "bfloat16"),
    "zero": ("sbuf", [128, CW], "float32"),
}
SEMAPHORES = ["ld_x", "ld_w01", "ld_w2", "fill", "left", "in_w"]
for _c in range(NC):
    for _n in ("ps0", "ps1", "ps1q"):
        SCRATCH["%s_%d" % (_n, _c)] = ("psum", [128, 512], "float32")
    for _n in ("in_x", "in_h1", "in_h2", "mm0", "mm1", "mm1q", "mm2", "ok_h1", "ok_h2", "ok_h2q", "ok_y", "st_y"):
        SEMAPHORES.append("%s_%d" % (_n, _c))


def _count(mask):
    n = 0
    while mask:
        n += mask & 1
        mask >>= 1
    return n


def rank_program(g, core, T, topo):
    r = T.rank_of(core)
    if r is None:
        return
    cores, S = T.cores, T.sem
    near, side, far = cores[r ^ 1], cores[r ^ 2], cores[r ^ 4]
    assert not topo.may_write(far, core)
    fed = cores[r ^ 4 ^ 2]
    assert topo.may_write(core, fed) and topo.may_write(core, side) and topo.may_write(core, near)

    m_side, m_fed = topo.mask(core, side), topo.mask(core, fed)
    m_near = topo.mask(core, near) & m_side
    n_near, n_side, n_fed = _count(m_near), _count(m_side), _count(m_fed)

    def send(dst, out, src, sem, mask):
        rid, pid = topo.addr(dst, core)
        g.remote_dma(out_ap=out, in_ap=src, remote_sem=sem, local_sem=S.left, pid=pid, routing_id=rid,
                     dma_engine_mask=mask)

    def W(k):
        return T.ws[:, k * TK:(k + 1) * TK]

    def sem(name, c):
        return S["%s_%d" % (name, c)]

    def col(t, c):
        return t[:, c * CW:(c + 1) * CW]

    def ps(name, c):
        return T["%s_%d" % (name, c)][:, 0:CW]

    te, ve = g.tensor, g.vector
    blocks = range(NC)

    g.sync.dma_start(T.xs[:], T.x[:]).then_inc(S.ld_x, 16)
    g.scalar.dma_start(T.ws[:, 0:4 * TK], T.w[:, 0:4 * TK]).then_inc(S.ld_w01, 16)
    g.sync.dma_start(T.ws[:, 4 * TK:6 * TK], T.w[:, 4 * TK:6 * TK]).then_inc(S.ld_w2, 16)
    ve.memset(T.zero[:], 0.0).then_inc(S.fill, 1)

    g.wait_ge(S.ld_x, 16)
    for c in blocks:
        send(near, col(T.p0, c), col(T.xs, c), sem("in_x", c), m_near)
    g.wait_ge(S.ld_w01, 16)
    send(side, T.wq[:], T.ws[:, 2 * TK:4 * TK], S.in_w, m_side)
    for c in blocks:
        g.wait_ge(sem("ok_h1", c), 1)
        send(side, col(T.p1, c), col(T.h1, c), sem("in_h1", c), m_side)
    for c in blocks:
        g.wait_ge(sem("ok_h2q", c), 1)
        send(fed, col(T.p2, c), col(T.h2q, c), sem("in_h2", c), m_fed)

    te.wait_ge(S.ld_x, 16)
    te.wait_ge(S.ld_w01, 16)
    for c in blocks:
        te.matmul(ps("ps0", c), W(0), col(T.xs, c), start=True, stop=False)
    for c in blocks:
        te.wait_ge(sem("in_x", c), n_near)
        te.matmul(ps("ps0", c), W(1), col(T.p0, c), start=False, stop=True).then_inc(sem("mm0", c), 1)

    for c in blocks:
        te.wait_ge(sem("ok_h1", c), 1)
        te.matmul(ps("ps1", c), W(2), col(T.h1, c), start=True, stop=False)
    te.wait_ge(S.in_w, n_side)
    for c in blocks:
        te.matmul(ps("ps1q", c), T.wq[:, TK:2 * TK], col(T.h1, c), start=True, stop=False)
    for c in blocks:
        te.wait_ge(sem("in_h1", c), n_side)
        te.matmul(ps("ps1q", c), T.wq[:, 0:TK], col(T.p1, c), start=False, stop=True).then_inc(sem("mm1q", c), 1)
        te.matmul(ps("ps1", c), W(3), col(T.p1, c), start=False, stop=True).then_inc(sem("mm1", c), 1)

    te.wait_ge(S.ld_w2, 16)
    for c in blocks:
        te.wait_ge(sem("ok_h2", c), 1)
        te.matmul(ps("ps0", c), W(4), col(T.h2, c), start=True, stop=False)
    for c in blocks:
        te.wait_ge(sem("in_h2", c), n_fed)
        te.matmul(ps("ps0", c), W(5), col(T.p2, c), start=False, stop=True).then_inc(sem("mm2", c), 1)

    def relu(mm, p, out, ok, c):
        ve.wait_ge(sem(mm, c), 1)
        ve.tensor_tensor(out=col(out, c), in0=ps(p, c), in1=T.zero[:], op=AluOpType.max).then_inc(sem(ok, c), 1)

    ve.wait_ge(S.fill, 1)
    for c in blocks:
        relu("mm0", "ps0", T.h1, "ok_h1", c)
    for c in blocks:
        relu("mm1q", "ps1q", T.h2q, "ok_h2q", c)
        relu("mm1", "ps1", T.h2, "ok_h2", c)
    for c in blocks:
        relu("mm2", "ps0", T.yb, "ok_y", c)

    for c in blocks:
        q = (g.sync, g.scalar)[c % 2]
        q.wait_ge(sem("ok_y", c), 1)
        q.dma_start(col(T.y, c), col(T.yb, c)).then_inc(sem("st_y", c), 16)
        q.wait_ge(sem("st_y", c), 16)
    g.wait_ge(S.left, NC * (n_near + n_side + n_fed) + n_side)
